import numpy as np
import ml_dtypes


def mxq(x, axis, fmt="e4m3"):
    dtype, down = {"e4m3": (ml_dtypes.float8_e4m3fn, 7), "e5m2": (ml_dtypes.float8_e5m2, 14)}[fmt]
    v = np.moveaxis(np.asarray(x, np.float32).astype(ml_dtypes.bfloat16).astype(np.float64), axis, -1)
    blocks = v.reshape(v.shape[:-1] + (-1, 32))
    amax = np.abs(blocks).max(-1, keepdims=True)
    byte = np.maximum(np.where(amax > 0, np.frexp(amax)[1] - 1 + 127, 0) - down, 1)
    scale = np.exp2(byte - 127.0)
    codes = (blocks / scale).astype(np.float32).astype(dtype).astype(np.float64)
    return np.moveaxis((codes * scale).reshape(v.shape), -1, axis)


WIDE = False


def mx_kscale(k):
    if not WIDE:
        return np.ones(k)
    levels = np.array([10, -10, 5, -5, 0])
    if k % 512:
        return np.exp2(np.random.permutation(np.resize(levels, k // 32))).repeat(32)
    a = np.empty((k // 512, 16))
    for p in range(k // 512):
        a[p, :8] = np.random.permutation(np.resize(levels, 8))
        for g in range(8):
            far = levels[np.abs(levels - a[p, g]) >= 10]
            a[p, g + 8] = far[np.random.randint(len(far))]
    return np.exp2(a.ravel()).repeat(32)


BF16 = ml_dtypes.bfloat16


def bf(x):
    return np.asarray(x, np.float32).astype(BF16)


def f64(x):
    return np.asarray(x).astype(np.float64)


E2M1 = np.array([0.0, 0.5, 1.0, 1.5, 2.0, 3.0, 4.0, 6.0, -0.0, -0.5, -1.0, -1.5, -2.0, -3.0, -4.0, -6.0])


def pack_weight(w, fmt):
    k, n = w.shape
    w = f64(bf(w)).reshape(k // 32, 32, n)
    amax = np.abs(w).max(1)
    if fmt == "e4m3":
        byte = np.frexp(amax)[1] - 1 + 127 - 7
    else:
        mant, ex = np.frexp(amax / 6.0)
        byte = np.where(mant > 0.5, ex, ex - 1) + 127
    byte = np.clip(np.where(amax > 0, byte, 1), 1, 254)
    scaled = (w * np.exp2(127.0 - byte)[:, None, :]).reshape(k, n).astype(np.float32)
    by_word = np.ascontiguousarray(scaled.reshape(k // 512, 128, 4, n).transpose(0, 1, 3, 2))
    if fmt == "e4m3":
        words = by_word.astype(ml_dtypes.float8_e4m3fn).view(np.uint8)
    else:
        c = by_word.astype(ml_dtypes.float4_e2m1fn).view(np.uint8) & 0xF
        words = c[..., 0::2] | (c[..., 1::2] << 4)
    return np.ascontiguousarray(words), np.ascontiguousarray(byte.astype(np.uint8).reshape(k // 512, 16, n))


def unpack_weight(words, scales, fmt):
    g, p, n, _ = words.shape
    if fmt == "e4m3":
        vals = np.ascontiguousarray(words).view(ml_dtypes.float8_e4m3fn).astype(np.float64)
    else:
        nib = np.empty((g, p, n, 4), np.uint8)
        nib[..., 0::2] = words & 0xF
        nib[..., 1::2] = words >> 4
        vals = E2M1[nib]
    vals = vals * np.repeat(np.exp2(scales.astype(np.float64) - 127.0), 8, axis=1)[..., None]
    return vals.transpose(0, 1, 3, 2).reshape(g * 512, n)
def pack4(w):
    words, scales = pack_weight(w, "e2m1")
    return words.reshape(words.shape[0], 128, -1), scales


def unpack4(words, scales):
    return unpack_weight(words.reshape(words.shape[0], 128, -1, 2), scales, "e2m1")


def planes(Y):
    n, m = Y.shape
    b = f64(bf(Y)).reshape(n // 32, 32, m)
    amax = np.abs(b).max(1)
    byte = np.clip(np.where(amax > 0, np.frexp(amax)[1] - 1 + 127 - 7, 1), 1, 254)
    codes = (b * np.exp2(127.0 - byte)[:, None, :]).reshape(n, m).astype(np.float32).astype(ml_dtypes.float8_e4m3fn).view(np.uint8)
    words = codes.reshape(n // 512, 128, 4, m).transpose(0, 1, 3, 2)
    return np.ascontiguousarray(words), np.ascontiguousarray(byte.astype(np.uint8).reshape(n // 512, 16, m))


M, K, N = 768, 1536, 2048


def setup_inputs():
    s_mean = mx_kscale(K)
    s_var = mx_kscale(K)
    mean = np.random.randn(M, K)
    var = 0.4 * np.exp(0.4 * np.random.randn(M, 1)) * np.exp(np.random.randn(M, K))
    w = np.random.randn(K, N) * np.exp(0.3 * np.random.randn(K, N)) / np.sqrt(K)
    w = w * np.exp(0.3 * np.random.randn(N))[None, :]
    proj_words, proj_scales = pack4(w / s_mean[:, None])
    sq_words, sq_scales = pack4(w * w / s_var[:, None])
    return {
        "mean": bf(mean * s_mean[None, :]),
        "var": bf(var * s_var[None, :]),
        "proj_words": proj_words,
        "proj_scales": proj_scales,
        "sq_words": sq_words,
        "sq_scales": sq_scales,
        "bias": bf(0.3 * np.random.randn(N)),
        "inv_target": bf(0.5 * np.exp(0.8 * np.random.randn(N))),
    }

def reference(mean, var, proj_words, proj_scales, sq_words, sq_scales, bias, inv_target):
    W = unpack4(proj_words, proj_scales)
    S = unpack4(sq_words, sq_scales)
    P = mxq(f64(mean), 1, "e4m3") @ W
    V = mxq(f64(var), 1, "e4m3") @ S
    mu = P + f64(bias)
    y = (mu * mu + V) * f64(inv_target)
    Y = y.T
    words, scales = planes(Y)
    return y, words, scales

@@ -1,0 +1,285 @@
+from contextlib import ExitStack
+
+import concourse.mybir as mybir
+from concourse.masks import make_identity
+
+M, K, N = 768, 1536, 2048
+FLOPS = 2 * 2 * M * K * N
+
+F32 = mybir.dt.float32
+BF16 = mybir.dt.bfloat16
+I32 = mybir.dt.int32
+U32 = mybir.dt.uint32
+U8 = mybir.dt.uint8
+FP8X4 = mybir.dt.float8_e4m3fn_x4
+FP4X4 = mybir.dt.float4_e2m1fn_x4
+ALU = mybir.AluOpType
+ACT = mybir.ActivationFunctionType
+
+P = 128
+K_PASS = 512
+PASSES = K // K_PASS
+N_GROUP = 512
+GROUPS = N // N_GROUP
+M_TILES = M // P
+UNITS = GROUPS * M_TILES
+IN_BANKS = M_TILES * PASSES
+LEAD = 1
+P_BANKS, V_BANKS, T_BANKS = 2, 3, 3
+
+
+def tile_projected_second_moment_ratio_g4_kernel(
+    tc, mean, var, proj_words, proj_scales, sq_words, sq_scales, bias, inv_target, out_0, out_1, out_2
+):
+    nc = tc.nc
+    with ExitStack() as ctx:
+        keep = ctx.enter_context(tc.tile_pool(name="keep", bufs=1))
+        work = ctx.enter_context(tc.tile_pool(name="work", bufs=4))
+        psum = ctx.enter_context(tc.psum_pool(name="psum", bufs=1))
+        ctx.enter_context(tc.manual_schedule())
+
+        ident = keep.tile([P, P], F32, name="ident")
+        warm = keep.tile([P, 8], F32, name="warm")
+        vec_cols = [keep.tile([P, N // P], BF16, name="vec_cols%d" % a) for a in range(2)]
+        vec_rows = [keep.tile([P, N], BF16, name="vec_rows%d" % a) for a in range(2)]
+        x_raw = [[keep.tile([P, K], BF16, name="x_raw%d_%d" % (m, a)) for a in range(2)] for m in range(M_TILES)]
+        x_codes = [keep.tile([P, 2 * P], U32, name="x_codes%d" % j, align_bytes=64) for j in range(IN_BANKS)]
+        x_scales = [keep.tile([P, 2 * P], U8, name="x_scales%d" % j, align_bytes=64) for j in range(IN_BANKS)]
+        w_words = [[keep.tile([P, PASSES, 2 * N_GROUP], U8, name="w_words%d_%d" % (a, g), align_bytes=64)
+                    for g in range(GROUPS)] for a in range(2)]
+        w_sc_first = [keep.tile([P, PASSES, N_GROUP], U8, name="w_sc_first%d" % a, align_bytes=64) for a in range(2)]
+        w_sc_rest = [keep.tile([P, PASSES, N - N_GROUP], U8, name="w_sc_rest%d" % a, align_bytes=64) for a in range(2)]
+        y = [keep.tile([P, N_GROUP], F32, name="y%d" % u) for u in range(UNITS)]
+        y_codes = keep.tile([P, GROUPS, M], U32, name="y_codes", align_bytes=64)
+        y_scales = keep.tile([P, GROUPS, M], U8, name="y_scales", align_bytes=64)
+
+        x_hbm = [mean, var]
+        words_hbm = [proj_words.bitcast(I32), sq_words.bitcast(I32)]
+        scales_hbm = [proj_scales.bitcast(I32), sq_scales.bitcast(I32)]
+        vec_hbm = [bias, inv_target]
+        codes_out = out_1.rearrange("g p m t -> g p (m t)").bitcast(I32)
+        scales_out = out_2.bitcast(I32)
+
+        state = {}
+        t_count = [0]
+
+        def t_bank():
+            k = t_count[0] % T_BANKS
+            t_count.append(t_count.pop() + 1)
+            return psum.tile([P, N_GROUP], F32, name="t_bank", tag="t%d" % k)
+
+        def load_x(m, a):
+            nc.sync.dma_start(out=x_raw[m][a][:], in_=x_hbm[a][m * P:(m + 1) * P, :])
+
+        def load_w(a, g):
+            nc.sync.dma_start(
+                out=w_words[a][g][:].bitcast(I32),
+                in_=words_hbm[a][:, :, g * 256:(g + 1) * 256].rearrange("k p w -> p k w"),
+            )
+
+        def load_w_scales(a, plane, c0, c1):
+            for q in range(4):
+                nc.sync.dma_start(
+                    out=plane[32 * q:32 * q + 4, :, :].bitcast(I32),
+                    in_=scales_hbm[a][:, 4 * q:4 * q + 4, c0 // 4:c1 // 4].rearrange("k r w -> r k w"),
+                )
+
+        def spread(a, half, bank):
+            cols = vec_cols[a][:].bitcast(F32)
+            for c in range(4):
+                col = cols[:, 4 * half + c:4 * half + c + 1].to_broadcast([P, P])
+                nc.tensor.transpose(bank[:, c * P:(c + 1) * P], col, ident[:])
+            rows = vec_rows[a][:].bitcast(F32).rearrange("q (p c) -> q p c", c=8)
+            nc.vector.tensor_copy(out=rows[:, :, 4 * half:4 * half + 4], in_=bank[:].rearrange("q (c p) -> q p c", c=4))
+
+        def interleave(dst, bank, chunks):
+            nc.scalar.copy(
+                out=dst.bitcast(F32).rearrange("p (c r u) -> p c r u", c=chunks, u=2),
+                in_=bank.rearrange("p (c u r) -> p c r u", c=chunks, u=2),
+            )
+
+        def turn_x(j):
+            bank = t_bank()
+            for c in range(2):
+                m, rest = divmod(2 * j + c, 2 * PASSES)
+                a, k = divmod(rest, PASSES)
+                words = x_raw[m][a][:].bitcast(F32)
+                for u in range(2):
+                    nc.tensor.transpose(
+                        bank[:, (2 * c + u) * P:(2 * c + u + 1) * P], words[:, 256 * k + u:256 * (k + 1):2], ident[:]
+                    )
+            grouped = work.tile([P, 2 * K_PASS], BF16, name="x_grouped", align_bytes=64)
+            interleave(grouped[:], bank[:], 2)
+            nc.vector.quantize_mx(out=x_codes[j][:].bitcast(FP8X4), scales=x_scales[j][:], in_=grouped[:])
+
+        def product(u, a):
+            g, m = divmod(u, M_TILES)
+            banks = (P_BANKS, V_BANKS)[a]
+            acc = psum.tile([P, N_GROUP], F32, name="acc", tag="acc%d_%d" % (a, u % banks))
+            for k in range(PASSES):
+                j, c = divmod((2 * m + a) * PASSES + k, 2)
+                if g == 0:
+                    w_scale = w_sc_first[a][:, k, :]
+                else:
+                    w_scale = w_sc_rest[a][:, k, (g - 1) * N_GROUP:g * N_GROUP]
+                nc.tensor.matmul_mx(
+                    out=acc[:],
+                    lhsT=x_codes[j][:, c * P:(c + 1) * P].bitcast(FP8X4),
+                    lhsT_scale=x_scales[j][:, c * P:(c + 1) * P],
+                    rhs=w_words[a][g][:, k, :].bitcast(FP4X4),
+                    rhs_scale=w_scale,
+                    start=(k == 0),
+                    stop=(k == PASSES - 1),
+                )
+            state[("acc", a, u)] = acc
+
+        def group_cols(u):
+            g = u // M_TILES
+            return slice(g * N_GROUP, (g + 1) * N_GROUP)
+
+        def add_bias(u):
+            mu = work.tile([P, N_GROUP], F32, name="mu")
+            nc.vector.tensor_tensor(out=mu[:], in0=state[("acc", 0, u)][:], in1=vec_rows[0][:, group_cols(u)], op=ALU.add)
+            state[("mu", u)] = mu
+
+        def square(u):
+            mu2 = work.tile([P, N_GROUP], F32, name="mu2")
+            nc.scalar.activation(out=mu2[:], in_=state[("mu", u)][:], func=ACT.Square)
+            state[("mu2", u)] = mu2
+
+        def add_var(u):
+            second = work.tile([P, N_GROUP], F32, name="second")
+            nc.vector.tensor_tensor(out=second[:], in0=state[("acc", 1, u)][:], in1=state[("mu2", u)][:], op=ALU.add)
+            state[("second", u)] = second
+
+        def ratio(u):
+            g, m = divmod(u, M_TILES)
+            nc.vector.tensor_tensor(out=y[u][:], in0=state[("second", u)][:], in1=vec_rows[1][:, group_cols(u)], op=ALU.mult)
+            state["stores"].append((out_0[m * P:(m + 1) * P, group_cols(u)], y[u][:]))
+
+        def round_y(u):
+            y16 = work.tile([P, N_GROUP], BF16, name="y16", bufs=6)
+            nc.scalar.copy(
+                out=y16[:].rearrange("p (u q e) -> p u q e", u=2, e=2),
+                in_=y[u][:].rearrange("p (q u e) -> p u q e", u=2, e=2),
+            )
+            state[("y16", u)] = y16
+
+        def turn_y(u0, count):
+            bank = t_bank()
+            for c in range(count):
+                words = state[("y16", u0 + c)][:].bitcast(F32)
+                for u in range(2):
+                    nc.tensor.transpose(bank[:, (2 * c + u) * P:(2 * c + u + 1) * P], words[:, u * P:(u + 1) * P], ident[:])
+            grouped = work.tile([P, count * N_GROUP], BF16, name="y_grouped", align_bytes=64)
+            interleave(grouped[:], bank[:, 0:count * 2 * P], count)
+            state[("yg", u0)] = grouped
+
+        def quantize_y(u0, count):
+            g, m = divmod(u0, M_TILES)
+            cols = slice(m * P, (m + count) * P)
+            nc.vector.quantize_mx(out=y_codes[:, g, cols].bitcast(FP8X4), scales=y_scales[:, g, cols], in_=state[("yg", u0)][:])
+            state["stores"].append((codes_out[g, :, cols], y_codes[:, g, cols].bitcast(I32)))
+
+        def store_scales(g0, g1):
+            for q in range(4):
+                state["stores"].append((
+                    scales_out[g0:g1, 4 * q:4 * q + 4, :].rearrange("g r w -> r g w"),
+                    y_scales[32 * q:32 * q + 4, g0:g1, :].bitcast(I32),
+                ))
+
+        def flush():
+            for dst, src in state["stores"]:
+                nc.sync.dma_start(out=dst, in_=src)
+            state["stores"].clear()
+
+        state["stores"] = []
+
+        make_identity(nc, ident[:])
+        nc.scalar.activation(out=warm[:, 0:1], in_=ident[:, 0:1], func=ACT.Square)
+        for a in range(2):
+            nc.vector.memset(w_sc_first[a][:].rearrange("p k n -> p (k n)").bitcast(I32), 0)
+        for a in range(2):
+            nc.gpsimd.memset(w_sc_rest[a][:].rearrange("p k n -> p (k n)").bitcast(I32), 0)
+        nc.sync.dma_start(out=vec_cols[0][:], in_=vec_hbm[0].rearrange("(p c) -> p c", p=P))
+        load_x(0, 0)
+        load_x(0, 1)
+        nc.sync.dma_start(out=vec_cols[1][:], in_=vec_hbm[1].rearrange("(p c) -> p c", p=P))
+        for a in range(2):
+            load_w_scales(a, w_sc_first[a], 0, N_GROUP)
+            load_w(a, 0)
+        for m in (1, 2):
+            load_x(m, 0)
+            load_x(m, 1)
+        for a in range(2):
+            load_w_scales(a, w_sc_rest[a], N_GROUP, N)
+        for m, g in ((3, 1), (4, 2), (5, 3)):
+            load_x(m, 0)
+            load_x(m, 1)
+            load_w(0, g)
+            load_w(1, g)
+
+        for half in range(2):
+            bank = psum.tile([P, N_GROUP], F32, name="bias_bank", tag="acc1_%d" % (half + 1))
+            spread(0, half, bank)
+        for j in range(PASSES):
+            turn_x(j)
+        for half in range(2):
+            bank = psum.tile([P, N_GROUP], F32, name="inv_bank", tag="acc1_%d" % (half + 1))
+            spread(1, half, bank)
+        product(0, 0)
+        product(0, 1)
+        add_bias(0)
+
+        turned = PASSES
+        for u in range(1, M_TILES):
+            upto = min(PASSES * (u + 1) + LEAD, IN_BANKS)
+            square(u - 1)
+            add_var(u - 1)
+            turn_x(turned)
+            ratio(u - 1)
+            for j in range(turned + 1, upto):
+                turn_x(j)
+            turned = upto
+            round_y(u - 1)
+            if u % 2 == 1 and u >= 3:
+                turn_y(u - 3, 2)
+                quantize_y(u - 3, 2)
+            product(u, 0)
+            product(u, 1)
+            add_bias(u)
+            flush()
+
+        square(M_TILES - 1)
+        for u in range(M_TILES, UNITS):
+            due = u % 2 == 1 and u - 5 >= 4
+            if due:
+                turn_y(u - 5, 2)
+            product(u, 0)
+            add_bias(u)
+            product(u, 1)
+            square(u)
+            if u > M_TILES:
+                ratio(u - 2)
+                round_y(u - 2)
+            if due:
+                quantize_y(u - 5, 2)
+                if u - 4 == 3 * M_TILES - 1:
+                    store_scales(0, 3)
+            add_var(u - 1)
+            flush()
+
+        last = UNITS - 1
+        turn_y(last - 3, 2)
+        add_var(last)
+        ratio(last - 1)
+        round_y(last - 1)
+        quantize_y(last - 3, 2)
+        ratio(last)
+        round_y(last)
+        turn_y(last - 1, 1)
+        quantize_y(last - 1, 1)
+        turn_y(last, 1)
+        quantize_y(last, 1)
+        store_scales(3, 4)
+        flush()

@@ -24,8 +24,10 @@ GROUPS = N // N_GROUP
 M_TILES = M // P
 UNITS = GROUPS * M_TILES
 IN_BANKS = M_TILES * PASSES
-LEAD = 1
-P_BANKS, V_BANKS, T_BANKS = 2, 3, 3
+T_BANKS = 4
+STEPS = UNITS // 2
+IN_RUNS = {2: 2, 3: 2, 4: 2, 5: 2, 6: 2, 7: 1, 8: 1}
+POOL_STEPS = ()
 
 
 def tile_projected_second_moment_ratio_g4_kernel(
@@ -47,11 +49,11 @@ def tile_projected_second_moment_ratio_g4_kernel(
         x_scales = [keep.tile([P, 2 * P], U8, name="x_scales%d" % j, align_bytes=64) for j in range(IN_BANKS)]
         w_words = [[keep.tile([P, PASSES, 2 * N_GROUP], U8, name="w_words%d_%d" % (a, g), align_bytes=64)
                     for g in range(GROUPS)] for a in range(2)]
-        w_sc_first = [keep.tile([P, PASSES, N_GROUP], U8, name="w_sc_first%d" % a, align_bytes=64) for a in range(2)]
-        w_sc_rest = [keep.tile([P, PASSES, N - N_GROUP], U8, name="w_sc_rest%d" % a, align_bytes=64) for a in range(2)]
+        w_scales = [[keep.tile([P, PASSES, N_GROUP], U8, name="w_scales%d_%d" % (a, g), align_bytes=64)
+                     for g in range(GROUPS)] for a in range(2)]
         y = [keep.tile([P, N_GROUP], F32, name="y%d" % u) for u in range(UNITS)]
         y_codes = keep.tile([P, GROUPS, M], U32, name="y_codes", align_bytes=64)
-        y_scales = keep.tile([P, GROUPS, M], U8, name="y_scales", align_bytes=64)
+        y_scales = [keep.tile([P, GROUPS, 2 * P], U8, name="y_scales%d" % i, align_bytes=64) for i in range(M_TILES // 2)]
 
         x_hbm = [mean, var]
         words_hbm = [proj_words.bitcast(I32), sq_words.bitcast(I32)]
@@ -72,25 +74,32 @@ def tile_projected_second_moment_ratio_g4_kernel(
             nc.sync.dma_start(out=x_raw[m][a][:], in_=x_hbm[a][m * P:(m + 1) * P, :])
 
         def load_w(a, g):
+            for q in range(4):
+                nc.sync.dma_start(
+                    out=w_scales[a][g][32 * q:32 * q + 4, :, :].bitcast(I32),
+                    in_=scales_hbm[a][:, 4 * q:4 * q + 4, g * 128:(g + 1) * 128].rearrange("k r w -> r k w"),
+                )
             nc.sync.dma_start(
                 out=w_words[a][g][:].bitcast(I32),
                 in_=words_hbm[a][:, :, g * 256:(g + 1) * 256].rearrange("k p w -> p k w"),
             )
 
-        def load_w_scales(a, plane, c0, c1):
-            for q in range(4):
-                nc.sync.dma_start(
-                    out=plane[32 * q:32 * q + 4, :, :].bitcast(I32),
-                    in_=scales_hbm[a][:, 4 * q:4 * q + 4, c0 // 4:c1 // 4].rearrange("k r w -> r k w"),
-                )
+        def unit(u):
+            pair, g = divmod(u // 2, GROUPS)
+            return g, 2 * pair + u % 2
 
         def spread(a, half, bank):
+            state[("vec", a, half)] = bank
             cols = vec_cols[a][:].bitcast(F32)
             for c in range(4):
                 col = cols[:, 4 * half + c:4 * half + c + 1].to_broadcast([P, P])
                 nc.tensor.transpose(bank[:, c * P:(c + 1) * P], col, ident[:])
+
+        def spread_out(a, half):
+            bank = state[("vec", a, half)]
             rows = vec_rows[a][:].bitcast(F32).rearrange("q (p c) -> q p c", c=8)
-            nc.vector.tensor_copy(out=rows[:, :, 4 * half:4 * half + 4], in_=bank[:].rearrange("q (c p) -> q p c", c=4))
+            copy = nc.scalar.copy if a == 0 else nc.vector.tensor_copy
+            copy(out=rows[:, :, 4 * half:4 * half + 4], in_=bank[:].rearrange("q (c p) -> q p c", c=4))
 
         def interleave(dst, bank, chunks):
             nc.scalar.copy(
@@ -101,40 +110,39 @@ def tile_projected_second_moment_ratio_g4_kernel(
         def turn_x(j):
             bank = t_bank()
             for c in range(2):
-                m, rest = divmod(2 * j + c, 2 * PASSES)
-                a, k = divmod(rest, PASSES)
-                words = x_raw[m][a][:].bitcast(F32)
+                pair, rest = divmod(2 * j + c, 4 * PASSES)
+                a, rest = divmod(rest, 2 * PASSES)
+                i, k = divmod(rest, PASSES)
+                words = x_raw[2 * pair + i][a][:].bitcast(F32)
                 for u in range(2):
                     nc.tensor.transpose(
                         bank[:, (2 * c + u) * P:(2 * c + u + 1) * P], words[:, 256 * k + u:256 * (k + 1):2], ident[:]
                     )
             grouped = work.tile([P, 2 * K_PASS], BF16, name="x_grouped", align_bytes=64)
             interleave(grouped[:], bank[:], 2)
-            nc.vector.quantize_mx(out=x_codes[j][:].bitcast(FP8X4), scales=x_scales[j][:], in_=grouped[:])
+            state[("xg", j)] = grouped
+
+        def quantize_x(j):
+            nc.vector.quantize_mx(out=x_codes[j][:].bitcast(FP8X4), scales=x_scales[j][:], in_=state[("xg", j)][:])
 
         def product(u, a):
-            g, m = divmod(u, M_TILES)
-            banks = (P_BANKS, V_BANKS)[a]
-            acc = psum.tile([P, N_GROUP], F32, name="acc", tag="acc%d_%d" % (a, u % banks))
+            g, m = unit(u)
+            acc = psum.tile([P, N_GROUP], F32, name="acc", tag="acc%d_%d" % (a, u % 2))
             for k in range(PASSES):
-                j, c = divmod((2 * m + a) * PASSES + k, 2)
-                if g == 0:
-                    w_scale = w_sc_first[a][:, k, :]
-                else:
-                    w_scale = w_sc_rest[a][:, k, (g - 1) * N_GROUP:g * N_GROUP]
+                j, c = divmod(((m // 2 * 2 + a) * 2 + m % 2) * PASSES + k, 2)
                 nc.tensor.matmul_mx(
                     out=acc[:],
                     lhsT=x_codes[j][:, c * P:(c + 1) * P].bitcast(FP8X4),
                     lhsT_scale=x_scales[j][:, c * P:(c + 1) * P],
                     rhs=w_words[a][g][:, k, :].bitcast(FP4X4),
-                    rhs_scale=w_scale,
+                    rhs_scale=w_scales[a][g][:, k, :],
                     start=(k == 0),
                     stop=(k == PASSES - 1),
                 )
             state[("acc", a, u)] = acc
 
         def group_cols(u):
-            g = u // M_TILES
+            g = unit(u)[0]
             return slice(g * N_GROUP, (g + 1) * N_GROUP)
 
         def add_bias(u):
@@ -153,8 +161,9 @@ def tile_projected_second_moment_ratio_g4_kernel(
             state[("second", u)] = second
 
         def ratio(u):
-            g, m = divmod(u, M_TILES)
-            nc.vector.tensor_tensor(out=y[u][:], in0=state[("second", u)][:], in1=vec_rows[1][:, group_cols(u)], op=ALU.mult)
+            g, m = unit(u)
+            engine = nc.gpsimd if u // 2 in POOL_STEPS else nc.vector
+            engine.tensor_tensor(out=y[u][:], in0=state[("second", u)][:], in1=vec_rows[1][:, group_cols(u)], op=ALU.mult)
             state["stores"].append((out_0[m * P:(m + 1) * P, group_cols(u)], y[u][:]))
 
         def round_y(u):
@@ -164,6 +173,37 @@ def tile_projected_second_moment_ratio_g4_kernel(
                 in_=y[u][:].rearrange("p (q u e) -> p u q e", u=2, e=2),
             )
             state[("y16", u)] = y16
+
+        def by_word_parity(ap):
+            return ap.rearrange("p (q u e) -> p u q e", u=2, e=2)
+
+        def finish_last(u):
+            g, m = unit(u)
+            second = work.tile([P, 2, P, 2], F32, name="second")
+            y16 = work.tile([P, N_GROUP], BF16, name="y16", bufs=6)
+            inv = vec_rows[1][:, group_cols(u)]
+            for h in range(2):
+                nc.vector.tensor_tensor(
+                    out=second[:, h], in0=by_word_parity(state[("acc", 1, u)][:])[:, h],
+                    in1=by_word_parity(state[("mu2", u)][:])[:, h], op=ALU.add,
+                )
+            for h in range(2):
+                nc.vector.tensor_tensor(
+                    out=y16[:].rearrange("p (u q e) -> p u q e", u=2, e=2)[:, h],
+                    in0=second[:, h], in1=by_word_parity(inv)[:, h], op=ALU.mult,
+                )
+            state[("second", u)] = second
+            state[("y16", u)] = y16
+
+        def ratio_last(u):
+            g, m = unit(u)
+            nc.vector.tensor_tensor(
+                out=y[u][:].rearrange("p (q u e) -> p q u e", u=2, e=2),
+                in0=state[("second", u)][:].rearrange("p u q e -> p q u e"),
+                in1=vec_rows[1][:, group_cols(u)].rearrange("p (q u e) -> p q u e", u=2, e=2),
+                op=ALU.mult,
+            )
+            state["stores"].append((out_0[m * P:(m + 1) * P, group_cols(u)], y[u][:]))
 
         def turn_y(u0, count):
             bank = t_bank()
@@ -176,17 +216,18 @@ def tile_projected_second_moment_ratio_g4_kernel(
             state[("yg", u0)] = grouped
 
         def quantize_y(u0, count):
-            g, m = divmod(u0, M_TILES)
+            g, m = unit(u0)
             cols = slice(m * P, (m + count) * P)
-            nc.vector.quantize_mx(out=y_codes[:, g, cols].bitcast(FP8X4), scales=y_scales[:, g, cols], in_=state[("yg", u0)][:])
+            nc.vector.quantize_mx(out=y_codes[:, g, cols].bitcast(FP8X4), scales=y_scales[m // 2][:, g, (m % 2) * P:(m % 2 + count) * P], in_=state[("yg", u0)][:])
             state["stores"].append((codes_out[g, :, cols], y_codes[:, g, cols].bitcast(I32)))
 
-        def store_scales(g0, g1):
+        def store_scales(pair, engines):
+            words = slice(pair * 2 * P // 4, (pair + 1) * 2 * P // 4)
             for q in range(4):
-                state["stores"].append((
-                    scales_out[g0:g1, 4 * q:4 * q + 4, :].rearrange("g r w -> r g w"),
-                    y_scales[32 * q:32 * q + 4, g0:g1, :].bitcast(I32),
-                ))
+                engines[q % len(engines)].dma_start(
+                    out=scales_out[:, 4 * q:4 * q + 4, words].rearrange("g r w -> r g w"),
+                    in_=y_scales[pair][32 * q:32 * q + 4, :, :].bitcast(I32),
+                )
 
         def flush():
             for dst, src in state["stores"]:
@@ -197,89 +238,93 @@ def tile_projected_second_moment_ratio_g4_kernel(
 
         make_identity(nc, ident[:])
         nc.scalar.activation(out=warm[:, 0:1], in_=ident[:, 0:1], func=ACT.Square)
-        for a in range(2):
-            nc.vector.memset(w_sc_first[a][:].rearrange("p k n -> p (k n)").bitcast(I32), 0)
-        for a in range(2):
-            nc.gpsimd.memset(w_sc_rest[a][:].rearrange("p k n -> p (k n)").bitcast(I32), 0)
+        for g in range(GROUPS):
+            for a in range(2):
+                engine = nc.vector if g == 0 else nc.gpsimd
+                engine.memset(w_scales[a][g][:].rearrange("p k n -> p (k n)").bitcast(I32), 0)
         nc.sync.dma_start(out=vec_cols[0][:], in_=vec_hbm[0].rearrange("(p c) -> p c", p=P))
         load_x(0, 0)
-        load_x(0, 1)
+        load_x(1, 0)
         nc.sync.dma_start(out=vec_cols[1][:], in_=vec_hbm[1].rearrange("(p c) -> p c", p=P))
+        load_w(0, 0)
+        load_x(0, 1)
+        load_x(1, 1)
+        load_w(1, 0)
+        load_w(0, 1)
+        load_w(1, 1)
+        load_x(2, 0)
+        load_x(3, 0)
+        load_w(0, 2)
+        load_w(1, 2)
+        load_x(2, 1)
+        load_x(3, 1)
+        load_w(0, 3)
+        load_w(1, 3)
         for a in range(2):
-            load_w_scales(a, w_sc_first[a], 0, N_GROUP)
-            load_w(a, 0)
-        for m in (1, 2):
-            load_x(m, 0)
-            load_x(m, 1)
-        for a in range(2):
-            load_w_scales(a, w_sc_rest[a], N_GROUP, N)
-        for m, g in ((3, 1), (4, 2), (5, 3)):
-            load_x(m, 0)
-            load_x(m, 1)
-            load_w(0, g)
-            load_w(1, g)
+            load_x(4, a)
+            load_x(5, a)
 
-        for half in range(2):
-            bank = psum.tile([P, N_GROUP], F32, name="bias_bank", tag="acc1_%d" % (half + 1))
-            spread(0, half, bank)
         for j in range(PASSES):
             turn_x(j)
+            quantize_x(j)
         for half in range(2):
-            bank = psum.tile([P, N_GROUP], F32, name="inv_bank", tag="acc1_%d" % (half + 1))
-            spread(1, half, bank)
-        product(0, 0)
-        product(0, 1)
-        add_bias(0)
+            bank = psum.tile([P, N_GROUP], F32, name="bias_bank", tag="acc1_%d" % half)
+            spread(0, half, bank)
+            spread_out(0, half)
 
-        turned = PASSES
-        for u in range(1, M_TILES):
-            upto = min(PASSES * (u + 1) + LEAD, IN_BANKS)
-            square(u - 1)
-            add_var(u - 1)
-            turn_x(turned)
-            ratio(u - 1)
-            for j in range(turned + 1, upto):
-                turn_x(j)
-            turned = upto
-            round_y(u - 1)
-            if u % 2 == 1 and u >= 3:
-                turn_y(u - 3, 2)
-                quantize_y(u - 3, 2)
-            product(u, 0)
-            product(u, 1)
-            add_bias(u)
-            flush()
-
-        square(M_TILES - 1)
-        for u in range(M_TILES, UNITS):
-            due = u % 2 == 1 and u - 5 >= 4
-            if due:
-                turn_y(u - 5, 2)
+        turned = 2 * PASSES
+        for s in range(STEPS):
+            u = 2 * s
+            last = s == STEPS - 1
             product(u, 0)
             add_bias(u)
-            product(u, 1)
             square(u)
-            if u > M_TILES:
-                ratio(u - 2)
-                round_y(u - 2)
-            if due:
-                quantize_y(u - 5, 2)
-                if u - 4 == 3 * M_TILES - 1:
-                    store_scales(0, 3)
-            add_var(u - 1)
-            flush()
-
-        last = UNITS - 1
-        turn_y(last - 3, 2)
-        add_var(last)
-        ratio(last - 1)
-        round_y(last - 1)
-        quantize_y(last - 3, 2)
-        ratio(last)
-        round_y(last)
-        turn_y(last - 1, 1)
-        quantize_y(last - 1, 1)
-        turn_y(last, 1)
-        quantize_y(last, 1)
-        store_scales(3, 4)
-        flush()
+            if s == 0:
+                for j in (PASSES, PASSES + 1):
+                    turn_x(j)
+                    quantize_x(j)
+            product(u + 1, 0)
+            add_bias(u + 1)
+            if s == 0:
+                turn_x(PASSES + 2)
+                quantize_x(PASSES + 2)
+                for half in range(2):
+                    spread(1, half, t_bank())
+                    spread_out(1, half)
+            square(u + 1)
+            if s >= 2:
+                quantize_y(u - 4, 2)
+            product(u, 1)
+            add_var(u)
+            if last:
+                turn_y(u - 2, 2)
+                ratio(u)
+                round_y(u)
+                product(u + 1, 1)
+                finish_last(u + 1)
+                turn_y(u, 1)
+                turn_y(u + 1, 1)
+                quantize_y(u - 2, 2)
+                ratio_last(u + 1)
+                quantize_y(u, 1)
+                quantize_y(u + 1, 1)
+                flush()
+                store_scales(2, (nc.scalar, nc.sync))
+            else:
+                product(u + 1, 1)
+                add_var(u + 1)
+                banks = range(turned, turned + IN_RUNS.get(s + 1, 0))
+                turned = turned + len(banks)
+                for j in banks:
+                    turn_x(j)
+                if s >= 1:
+                    turn_y(u - 2, 2)
+                ratio(u)
+                ratio(u + 1)
+                for j in banks:
+                    quantize_x(j)
+                round_y(u)
+                round_y(u + 1)
+                flush()
+                if s in (GROUPS + 1, 2 * GROUPS + 1):
+                    store_scales(s // GROUPS - 1, (nc.sync,))

@@ -23,11 +23,25 @@ N_GROUP = 512
 GROUPS = N // N_GROUP
 M_TILES = M // P
 UNITS = GROUPS * M_TILES
-IN_BANKS = M_TILES * PASSES
 T_BANKS = 4
 STEPS = UNITS // 2
-IN_RUNS = {2: 2, 3: 2, 4: 2, 5: 2, 6: 2, 7: 1, 8: 1}
-POOL_STEPS = ()
+IN_RUNS = {2: 2, 3: 2, 4: 2, 5: 1, 6: 2, 7: 2, 8: 1}
+POOL_UNITS = ()
+SPLIT = 3
+SORT_STEP = {(2, 1): 2, (3, 1): 2, (4, 0): 3, (5, 0): 4, (4, 1): 5, (5, 1): 6}
+SORT_ENG = "av"
+SORT_HEAD = ((1, 0), (0, 1), (1, 1))
+TIERS = ((0, 1), (1, 2), (2, 4))
+MERGE_O = 0
+HEAD = 0
+TAIL = 0
+MERGE = 1
+SC_POOL = 0
+
+
+def input_banks():
+    chunks = [(2 * pair + i, a, k) for pair in range(M_TILES // 2) for a in range(2) for i in range(2) for k in range(PASSES)]
+    return [chunks[j:j + 2] for j in range(0, len(chunks), 2)]
 
 
 def tile_projected_second_moment_ratio_g4_kernel(
@@ -45,12 +59,16 @@ def tile_projected_second_moment_ratio_g4_kernel(
         vec_cols = [keep.tile([P, N // P], BF16, name="vec_cols%d" % a) for a in range(2)]
         vec_rows = [keep.tile([P, N], BF16, name="vec_rows%d" % a) for a in range(2)]
         x_raw = [[keep.tile([P, K], BF16, name="x_raw%d_%d" % (m, a)) for a in range(2)] for m in range(M_TILES)]
-        x_codes = [keep.tile([P, 2 * P], U32, name="x_codes%d" % j, align_bytes=64) for j in range(IN_BANKS)]
-        x_scales = [keep.tile([P, 2 * P], U8, name="x_scales%d" % j, align_bytes=64) for j in range(IN_BANKS)]
+        x_sorted = {}
+        banks_in = input_banks()
+        place = {chunk: (j, c) for j, chunks in enumerate(banks_in) for c, chunk in enumerate(chunks)}
+        x_codes = [keep.tile([P, len(b) * P], U32, name="x_codes%d" % j, align_bytes=64) for j, b in enumerate(banks_in)]
+        x_scales = [keep.tile([P, len(b) * P], U8, name="x_scales%d" % j, align_bytes=64) for j, b in enumerate(banks_in)]
         w_words = [[keep.tile([P, PASSES, 2 * N_GROUP], U8, name="w_words%d_%d" % (a, g), align_bytes=64)
                     for g in range(GROUPS)] for a in range(2)]
-        w_scales = [[keep.tile([P, PASSES, N_GROUP], U8, name="w_scales%d_%d" % (a, g), align_bytes=64)
-                     for g in range(GROUPS)] for a in range(2)]
+        w_scales = [[keep.tile([P, PASSES, (g1 - g0) * N_GROUP], U8, name="w_scales%d_%d" % (a, g0), align_bytes=64)
+                     for g0, g1 in TIERS] for a in range(2)]
+        tier_of = {g: t for t, (g0, g1) in enumerate(TIERS) for g in range(g0, g1)}
         y = [keep.tile([P, N_GROUP], F32, name="y%d" % u) for u in range(UNITS)]
         y_codes = keep.tile([P, GROUPS, M], U32, name="y_codes", align_bytes=64)
         y_scales = [keep.tile([P, GROUPS, 2 * P], U8, name="y_scales%d" % i, align_bytes=64) for i in range(M_TILES // 2)]
@@ -70,15 +88,22 @@ def tile_projected_second_moment_ratio_g4_kernel(
             t_count.append(t_count.pop() + 1)
             return psum.tile([P, N_GROUP], F32, name="t_bank", tag="t%d" % k)
 
-        def load_x(m, a):
-            nc.sync.dma_start(out=x_raw[m][a][:], in_=x_hbm[a][m * P:(m + 1) * P, :])
+        def load_x(m, a, k0=0, k1=PASSES):
+            cols = slice(k0 * K_PASS, k1 * K_PASS)
+            nc.sync.dma_start(out=x_raw[m][a][:, cols], in_=x_hbm[a][m * P:(m + 1) * P, cols])
 
-        def load_w(a, g):
+        def load_scales(a, t):
+            g0, g1 = TIERS[t]
+            plane = w_scales[a][t]
             for q in range(4):
                 nc.sync.dma_start(
-                    out=w_scales[a][g][32 * q:32 * q + 4, :, :].bitcast(I32),
-                    in_=scales_hbm[a][:, 4 * q:4 * q + 4, g * 128:(g + 1) * 128].rearrange("k r w -> r k w"),
+                    out=plane[32 * q:32 * q + 4, :, :].bitcast(I32),
+                    in_=scales_hbm[a][:, 4 * q:4 * q + 4, g0 * 128:g1 * 128].rearrange("k r w -> r k w"),
                 )
+
+        def load_w(a, g):
+            if TIERS[tier_of[g]][0] == g:
+                load_scales(a, tier_of[g])
             nc.sync.dma_start(
                 out=w_words[a][g][:].bitcast(I32),
                 in_=words_hbm[a][:, :, g * 256:(g + 1) * 256].rearrange("k p w -> p k w"),
@@ -98,7 +123,7 @@ def tile_projected_second_moment_ratio_g4_kernel(
         def spread_out(a, half):
             bank = state[("vec", a, half)]
             rows = vec_rows[a][:].bitcast(F32).rearrange("q (p c) -> q p c", c=8)
-            copy = nc.scalar.copy if a == 0 else nc.vector.tensor_copy
+            copy = nc.scalar.copy
             copy(out=rows[:, :, 4 * half:4 * half + 4], in_=bank[:].rearrange("q (c p) -> q p c", c=4))
 
         def interleave(dst, bank, chunks):
@@ -107,38 +132,51 @@ def tile_projected_second_moment_ratio_g4_kernel(
                 in_=bank.rearrange("p (c u r) -> p c r u", c=chunks, u=2),
             )
 
+        def sort_words(m, a, engines):
+            out = work.tile([P, 2, PASSES, P], F32, name="x_sorted")
+            words = x_raw[m][a][:].bitcast(F32).rearrange("p (k q u) -> p u k q", k=PASSES, u=2)
+            if engines == "vv":
+                nc.vector.tensor_copy(out=out[:], in_=words)
+            elif engines == "aa":
+                nc.scalar.copy(out=out[:], in_=words)
+            else:
+                nc.scalar.copy(out=out[:, 0], in_=words[:, 0])
+                nc.vector.tensor_copy(out=out[:, 1], in_=words[:, 1])
+            x_sorted[(m, a)] = out
+
         def turn_x(j):
             bank = t_bank()
-            for c in range(2):
-                pair, rest = divmod(2 * j + c, 4 * PASSES)
-                a, rest = divmod(rest, 2 * PASSES)
-                i, k = divmod(rest, PASSES)
-                words = x_raw[2 * pair + i][a][:].bitcast(F32)
+            count = len(banks_in[j])
+            for c, (m, a, k) in enumerate(banks_in[j]):
+                words = x_raw[m][a][:].bitcast(F32)
                 for u in range(2):
-                    nc.tensor.transpose(
-                        bank[:, (2 * c + u) * P:(2 * c + u + 1) * P], words[:, 256 * k + u:256 * (k + 1):2], ident[:]
-                    )
-            grouped = work.tile([P, 2 * K_PASS], BF16, name="x_grouped", align_bytes=64)
-            interleave(grouped[:], bank[:], 2)
+                    src = x_sorted[(m, a)][:, u, k, :] if (m, a) in x_sorted else words[:, 256 * k + u:256 * (k + 1):2]
+                    nc.tensor.transpose(bank[:, (2 * c + u) * P:(2 * c + u + 1) * P], src, ident[:])
+            grouped = work.tile([P, count * K_PASS], BF16, name="x_grouped", align_bytes=64)
+            interleave(grouped[:], bank[:, 0:count * 2 * P], count)
             state[("xg", j)] = grouped
 
         def quantize_x(j):
             nc.vector.quantize_mx(out=x_codes[j][:].bitcast(FP8X4), scales=x_scales[j][:], in_=state[("xg", j)][:])
 
-        def product(u, a):
+        def passes(u, a, acc, n0, width):
             g, m = unit(u)
-            acc = psum.tile([P, N_GROUP], F32, name="acc", tag="acc%d_%d" % (a, u % 2))
+            s0 = (g - TIERS[tier_of[g]][0]) * N_GROUP + n0
             for k in range(PASSES):
-                j, c = divmod(((m // 2 * 2 + a) * 2 + m % 2) * PASSES + k, 2)
+                j, c = place[(m, a, k)]
                 nc.tensor.matmul_mx(
-                    out=acc[:],
+                    out=acc,
                     lhsT=x_codes[j][:, c * P:(c + 1) * P].bitcast(FP8X4),
                     lhsT_scale=x_scales[j][:, c * P:(c + 1) * P],
-                    rhs=w_words[a][g][:, k, :].bitcast(FP4X4),
-                    rhs_scale=w_scales[a][g][:, k, :],
+                    rhs=w_words[a][g][:, k, 2 * n0:2 * (n0 + width)].bitcast(FP4X4),
+                    rhs_scale=w_scales[a][tier_of[g]][:, k, s0:s0 + width],
                     start=(k == 0),
                     stop=(k == PASSES - 1),
                 )
+
+        def product(u, a):
+            acc = psum.tile([P, N_GROUP], F32, name="acc", tag="acc%d_%d" % (a, u % 2))
+            passes(u, a, acc[:], 0, N_GROUP)
             state[("acc", a, u)] = acc
 
         def group_cols(u):
@@ -162,7 +200,7 @@ def tile_projected_second_moment_ratio_g4_kernel(
 
         def ratio(u):
             g, m = unit(u)
-            engine = nc.gpsimd if u // 2 in POOL_STEPS else nc.vector
+            engine = nc.gpsimd if u in POOL_UNITS else nc.vector
             engine.tensor_tensor(out=y[u][:], in0=state[("second", u)][:], in1=vec_rows[1][:, group_cols(u)], op=ALU.mult)
             state["stores"].append((out_0[m * P:(m + 1) * P, group_cols(u)], y[u][:]))
 
@@ -210,7 +248,8 @@ def tile_projected_second_moment_ratio_g4_kernel(
             for c in range(count):
                 words = state[("y16", u0 + c)][:].bitcast(F32)
                 for u in range(2):
-                    nc.tensor.transpose(bank[:, (2 * c + u) * P:(2 * c + u + 1) * P], words[:, u * P:(u + 1) * P], ident[:])
+                    src = words[:, u * P:(u + 1) * P]
+                    nc.tensor.transpose(bank[:, (2 * c + u) * P:(2 * c + u + 1) * P], src, ident[:])
             grouped = work.tile([P, count * N_GROUP], BF16, name="y_grouped", align_bytes=64)
             interleave(grouped[:], bank[:, 0:count * 2 * P], count)
             state[("yg", u0)] = grouped
@@ -237,15 +276,16 @@ def tile_projected_second_moment_ratio_g4_kernel(
         state["stores"] = []
 
         make_identity(nc, ident[:])
-        nc.scalar.activation(out=warm[:, 0:1], in_=ident[:, 0:1], func=ACT.Square)
-        for g in range(GROUPS):
+        for first in range(len(TIERS)):
             for a in range(2):
-                engine = nc.vector if g == 0 else nc.gpsimd
-                engine.memset(w_scales[a][g][:].rearrange("p k n -> p (k n)").bitcast(I32), 0)
-        nc.sync.dma_start(out=vec_cols[0][:], in_=vec_hbm[0].rearrange("(p c) -> p c", p=P))
-        load_x(0, 0)
+                nc.vector.memset(w_scales[a][first][:].rearrange("p k n -> p (k n)").bitcast(I32), 0)
+        nc.scalar.activation(out=warm[:, 0:1], in_=ident[:, 0:1], func=ACT.Square)
+        for a in range(2):
+            nc.sync.dma_start(out=vec_cols[a][:], in_=vec_hbm[a].rearrange("(p c) -> p c", p=P))
+        load_x(0, 0, 0, SPLIT)
+        if SPLIT < PASSES:
+            load_x(0, 0, SPLIT, PASSES)
         load_x(1, 0)
-        nc.sync.dma_start(out=vec_cols[1][:], in_=vec_hbm[1].rearrange("(p c) -> p c", p=P))
         load_w(0, 0)
         load_x(0, 1)
         load_x(1, 1)
@@ -264,50 +304,81 @@ def tile_projected_second_moment_ratio_g4_kernel(
             load_x(4, a)
             load_x(5, a)
 
-        for j in range(PASSES):
-            turn_x(j)
-            quantize_x(j)
-        for half in range(2):
-            bank = psum.tile([P, N_GROUP], F32, name="bias_bank", tag="acc1_%d" % half)
-            spread(0, half, bank)
-            spread_out(0, half)
+        def turn_and_quantize(js):
+            for j in js:
+                turn_x(j)
+                quantize_x(j)
 
-        turned = 2 * PASSES
+        def head_sort(m, a):
+            if (m, a) in SORT_HEAD:
+                sort_words(m, a, "vv")
+
+        def spread_both(a, halves):
+            for half in halves:
+                if a == 0:
+                    bank = psum.tile([P, N_GROUP], F32, name="vec_bank", tag="acc1_%d" % half)
+                else:
+                    bank = t_bank()
+                spread(a, half, bank)
+                spread_out(a, half)
+
+        spread_both(0, (0,))
+        head_sort(0, 0)
+        head_sort(1, 0)
+        turn_and_quantize((0, 1))
+        head_sort(0, 1)
+        turn_and_quantize((2,))
+        product(0, 0)
+        head_sort(1, 1)
+        turn_and_quantize((3, 4))
+        spread_both(0, (1,))
+        product(1, 0)
+        turn_and_quantize((5,))
+        spread_both(1, (0,))
+        add_bias(0)
+        square(0)
+        add_bias(1)
+        square(1)
+        spread_both(1, (1,))
+
+        turned = 6
         for s in range(STEPS):
             u = 2 * s
             last = s == STEPS - 1
-            product(u, 0)
-            add_bias(u)
-            square(u)
-            if s == 0:
-                for j in (PASSES, PASSES + 1):
-                    turn_x(j)
-                    quantize_x(j)
-            product(u + 1, 0)
-            add_bias(u + 1)
-            if s == 0:
-                turn_x(PASSES + 2)
-                quantize_x(PASSES + 2)
-                for half in range(2):
-                    spread(1, half, t_bank())
-                    spread_out(1, half)
-            square(u + 1)
-            if s >= 2:
+            if s > 0:
+                product(u, 0)
+                add_bias(u)
+                square(u)
+                product(u + 1, 0)
+                add_bias(u + 1)
+                square(u + 1)
+            for tile_key, step in SORT_STEP.items():
+                if step == s:
+                    sort_words(tile_key[0], tile_key[1], SORT_ENG)
+            if s >= 2 and not last:
                 quantize_y(u - 4, 2)
             product(u, 1)
             add_var(u)
+            if last:
+                quantize_y(u - 4, 2)
             if last:
                 turn_y(u - 2, 2)
                 ratio(u)
                 round_y(u)
                 product(u + 1, 1)
                 finish_last(u + 1)
-                turn_y(u, 1)
-                turn_y(u + 1, 1)
+                if MERGE:
+                    turn_y(u, 2)
+                else:
+                    turn_y(u, 1)
+                    turn_y(u + 1, 1)
                 quantize_y(u - 2, 2)
                 ratio_last(u + 1)
-                quantize_y(u, 1)
-                quantize_y(u + 1, 1)
+                if MERGE:
+                    quantize_y(u, 2)
+                else:
+                    quantize_y(u, 1)
+                    quantize_y(u + 1, 1)
                 flush()
                 store_scales(2, (nc.scalar, nc.sync))
             else:

@@ -26,16 +26,18 @@ UNITS = GROUPS * M_TILES
 T_BANKS = 4
 STEPS = UNITS // 2
 IN_RUNS = {2: 2, 3: 2, 4: 2, 5: 1, 6: 2, 7: 2, 8: 1}
-POOL_UNITS = ()
-SPLIT = 3
-SORT_STEP = {(2, 1): 2, (3, 1): 2, (4, 0): 3, (5, 0): 4, (4, 1): 5, (5, 1): 6}
+POOL_UNITS = range(16, 22)
+SPLIT = 2
+SORT_STEP = {}
 SORT_ENG = "av"
-SORT_HEAD = ((1, 0), (0, 1), (1, 1))
+SORT_HEAD = ((1, 0), (0, 1))
+SPREAD_V = ((0, 0), (1, 0))
 TIERS = ((0, 1), (1, 2), (2, 4))
 MERGE_O = 0
-HEAD = 0
+HEAD = 1
 TAIL = 0
-MERGE = 1
+MERGE = 0
+QPOS = 2
 SC_POOL = 0
 
 
@@ -123,7 +125,7 @@ def tile_projected_second_moment_ratio_g4_kernel(
         def spread_out(a, half):
             bank = state[("vec", a, half)]
             rows = vec_rows[a][:].bitcast(F32).rearrange("q (p c) -> q p c", c=8)
-            copy = nc.scalar.copy
+            copy = nc.vector.tensor_copy if (a, half) in SPREAD_V else nc.scalar.copy
             copy(out=rows[:, :, 4 * half:4 * half + 4], in_=bank[:].rearrange("q (c p) -> q p c", c=4))
 
         def interleave(dst, bank, chunks):
@@ -325,77 +327,95 @@ def tile_projected_second_moment_ratio_g4_kernel(
         spread_both(0, (0,))
         head_sort(0, 0)
         head_sort(1, 0)
-        turn_and_quantize((0, 1))
+        turn_and_quantize((0,))
+        if HEAD == 1:
+            spread_both(0, (1,))
+        turn_and_quantize((1,))
         head_sort(0, 1)
         turn_and_quantize((2,))
+        if HEAD == 2:
+            spread_both(0, (1,))
         product(0, 0)
         head_sort(1, 1)
+        if HEAD:
+            add_bias(0)
         turn_and_quantize((3, 4))
-        spread_both(0, (1,))
+        if HEAD:
+            square(0)
+            spread_both(1, (0,))
+        else:
+            spread_both(0, (1,))
         product(1, 0)
+        if HEAD:
+            add_bias(1)
         turn_and_quantize((5,))
-        spread_both(1, (0,))
-        add_bias(0)
-        square(0)
-        add_bias(1)
-        square(1)
+        if HEAD:
+            square(1)
+        else:
+            spread_both(1, (0,))
+            add_bias(0)
+            square(0)
+            add_bias(1)
+            square(1)
         spread_both(1, (1,))
 
         turned = 6
+        banks = []
         for s in range(STEPS):
             u = 2 * s
             last = s == STEPS - 1
             if s > 0:
+                round_y(u - 2)
+                if u - 1 not in POOL_UNITS:
+                    round_y(u - 1)
                 product(u, 0)
                 add_bias(u)
                 square(u)
+                if u - 1 in POOL_UNITS:
+                    round_y(u - 1)
+                for j in banks[:QPOS]:
+                    quantize_x(j)
                 product(u + 1, 0)
                 add_bias(u + 1)
                 square(u + 1)
-            for tile_key, step in SORT_STEP.items():
-                if step == s:
-                    sort_words(tile_key[0], tile_key[1], SORT_ENG)
-            if s >= 2 and not last:
+                for j in banks[QPOS:]:
+                    quantize_x(j)
+            if s >= 2:
                 quantize_y(u - 4, 2)
             product(u, 1)
             add_var(u)
             if last:
-                quantize_y(u - 4, 2)
-            if last:
-                turn_y(u - 2, 2)
                 ratio(u)
-                round_y(u)
                 product(u + 1, 1)
-                finish_last(u + 1)
-                if MERGE:
-                    turn_y(u, 2)
+                if TAIL == 0:
+                    turn_y(u - 2, 2)
+                    round_y(u)
                 else:
-                    turn_y(u, 1)
-                    turn_y(u + 1, 1)
+                    round_y(u)
+                    turn_y(u - 2, 2)
+                finish_last(u + 1)
+                turn_y(u, 1)
+                turn_y(u + 1, 1)
                 quantize_y(u - 2, 2)
                 ratio_last(u + 1)
-                if MERGE:
-                    quantize_y(u, 2)
-                else:
-                    quantize_y(u, 1)
-                    quantize_y(u + 1, 1)
+                quantize_y(u, 1)
+                quantize_y(u + 1, 1)
                 flush()
                 store_scales(2, (nc.scalar, nc.sync))
             else:
+                if u in POOL_UNITS:
+                    ratio(u)
                 product(u + 1, 1)
                 add_var(u + 1)
-                banks = range(turned, turned + IN_RUNS.get(s + 1, 0))
+                if u not in POOL_UNITS:
+                    ratio(u)
+                ratio(u + 1)
+                banks = list(range(turned, turned + IN_RUNS.get(s + 1, 0)))
                 turned = turned + len(banks)
                 for j in banks:
                     turn_x(j)
                 if s >= 1:
                     turn_y(u - 2, 2)
-                ratio(u)
-                ratio(u + 1)
-                for j in banks:
-                    quantize_x(j)
-                round_y(u)
-                round_y(u + 1)
                 flush()
                 if s in (GROUPS + 1, 2 * GROUPS + 1):
                     store_scales(s // GROUPS - 1, (nc.sync,))

from contextlib import ExitStack

import concourse.mybir as mybir
from concourse.masks import make_identity

M, K, N = 768, 1536, 2048
FLOPS = 2 * 2 * M * K * N

F32 = mybir.dt.float32
BF16 = mybir.dt.bfloat16
I32 = mybir.dt.int32
U32 = mybir.dt.uint32
U8 = mybir.dt.uint8
FP8X4 = mybir.dt.float8_e4m3fn_x4
FP4X4 = mybir.dt.float4_e2m1fn_x4
ALU = mybir.AluOpType
ACT = mybir.ActivationFunctionType

P = 128
K_PASS = 512
PASSES = K // K_PASS
N_GROUP = 512
GROUPS = N // N_GROUP
M_TILES = M // P
UNITS = GROUPS * M_TILES
T_BANKS = 4
STEPS = UNITS // 2
IN_RUNS = {2: 2, 3: 2, 4: 2, 5: 1, 6: 2, 7: 2, 8: 1}
POOL_UNITS = range(16, 22)
SPLIT = 2
SORT_STEP = {}
SORT_ENG = "av"
SORT_HEAD = ((1, 0), (0, 1))
SPREAD_V = ((0, 0), (1, 0))
TIERS = ((0, 1), (1, 2), (2, 4))
MERGE_O = 0
HEAD = 1
TAIL = 0
MERGE = 0
QPOS = 2
SC_POOL = 0


def input_banks():
    chunks = [(2 * pair + i, a, k) for pair in range(M_TILES // 2) for a in range(2) for i in range(2) for k in range(PASSES)]
    return [chunks[j:j + 2] for j in range(0, len(chunks), 2)]


def tile_projected_second_moment_ratio_g4_kernel(
    tc, mean, var, proj_words, proj_scales, sq_words, sq_scales, bias, inv_target, out_0, out_1, out_2
):
    nc = tc.nc
    with ExitStack() as ctx:
        keep = ctx.enter_context(tc.tile_pool(name="keep", bufs=1))
        work = ctx.enter_context(tc.tile_pool(name="work", bufs=4))
        psum = ctx.enter_context(tc.psum_pool(name="psum", bufs=1))
        ctx.enter_context(tc.manual_schedule())

        ident = keep.tile([P, P], F32, name="ident")
        warm = keep.tile([P, 8], F32, name="warm")
        vec_cols = [keep.tile([P, N // P], BF16, name="vec_cols%d" % a) for a in range(2)]
        vec_rows = [keep.tile([P, N], BF16, name="vec_rows%d" % a) for a in range(2)]
        x_raw = [[keep.tile([P, K], BF16, name="x_raw%d_%d" % (m, a)) for a in range(2)] for m in range(M_TILES)]
        x_sorted = {}
        banks_in = input_banks()
        place = {chunk: (j, c) for j, chunks in enumerate(banks_in) for c, chunk in enumerate(chunks)}
        x_codes = [keep.tile([P, len(b) * P], U32, name="x_codes%d" % j, align_bytes=64) for j, b in enumerate(banks_in)]
        x_scales = [keep.tile([P, len(b) * P], U8, name="x_scales%d" % j, align_bytes=64) for j, b in enumerate(banks_in)]
        w_words = [[keep.tile([P, PASSES, 2 * N_GROUP], U8, name="w_words%d_%d" % (a, g), align_bytes=64)
                    for g in range(GROUPS)] for a in range(2)]
        w_scales = [[keep.tile([P, PASSES, (g1 - g0) * N_GROUP], U8, name="w_scales%d_%d" % (a, g0), align_bytes=64)
                     for g0, g1 in TIERS] for a in range(2)]
        tier_of = {g: t for t, (g0, g1) in enumerate(TIERS) for g in range(g0, g1)}
        y = [keep.tile([P, N_GROUP], F32, name="y%d" % u) for u in range(UNITS)]
        y_codes = keep.tile([P, GROUPS, M], U32, name="y_codes", align_bytes=64)
        y_scales = [keep.tile([P, GROUPS, 2 * P], U8, name="y_scales%d" % i, align_bytes=64) for i in range(M_TILES // 2)]

        x_hbm = [mean, var]
        words_hbm = [proj_words.bitcast(I32), sq_words.bitcast(I32)]
        scales_hbm = [proj_scales.bitcast(I32), sq_scales.bitcast(I32)]
        vec_hbm = [bias, inv_target]
        codes_out = out_1.rearrange("g p m t -> g p (m t)").bitcast(I32)
        scales_out = out_2.bitcast(I32)

        state = {}
        t_count = [0]

        def t_bank():
            k = t_count[0] % T_BANKS
            t_count.append(t_count.pop() + 1)
            return psum.tile([P, N_GROUP], F32, name="t_bank", tag="t%d" % k)

        def load_x(m, a, k0=0, k1=PASSES):
            cols = slice(k0 * K_PASS, k1 * K_PASS)
            nc.sync.dma_start(out=x_raw[m][a][:, cols], in_=x_hbm[a][m * P:(m + 1) * P, cols])

        def load_scales(a, t):
            g0, g1 = TIERS[t]
            plane = w_scales[a][t]
            for q in range(4):
                nc.sync.dma_start(
                    out=plane[32 * q:32 * q + 4, :, :].bitcast(I32),
                    in_=scales_hbm[a][:, 4 * q:4 * q + 4, g0 * 128:g1 * 128].rearrange("k r w -> r k w"),
                )

        def load_w(a, g):
            if TIERS[tier_of[g]][0] == g:
                load_scales(a, tier_of[g])
            nc.sync.dma_start(
                out=w_words[a][g][:].bitcast(I32),
                in_=words_hbm[a][:, :, g * 256:(g + 1) * 256].rearrange("k p w -> p k w"),
            )

        def unit(u):
            pair, g = divmod(u // 2, GROUPS)
            return g, 2 * pair + u % 2

        def spread(a, half, bank):
            state[("vec", a, half)] = bank
            cols = vec_cols[a][:].bitcast(F32)
            for c in range(4):
                col = cols[:, 4 * half + c:4 * half + c + 1].to_broadcast([P, P])
                nc.tensor.transpose(bank[:, c * P:(c + 1) * P], col, ident[:])

        def spread_out(a, half):
            bank = state[("vec", a, half)]
            rows = vec_rows[a][:].bitcast(F32).rearrange("q (p c) -> q p c", c=8)
            copy = nc.vector.tensor_copy if (a, half) in SPREAD_V else nc.scalar.copy
            copy(out=rows[:, :, 4 * half:4 * half + 4], in_=bank[:].rearrange("q (c p) -> q p c", c=4))

        def interleave(dst, bank, chunks):
            nc.scalar.copy(
                out=dst.bitcast(F32).rearrange("p (c r u) -> p c r u", c=chunks, u=2),
                in_=bank.rearrange("p (c u r) -> p c r u", c=chunks, u=2),
            )

        def sort_words(m, a, engines):
            out = work.tile([P, 2, PASSES, P], F32, name="x_sorted")
            words = x_raw[m][a][:].bitcast(F32).rearrange("p (k q u) -> p u k q", k=PASSES, u=2)
            if engines == "vv":
                nc.vector.tensor_copy(out=out[:], in_=words)
            elif engines == "aa":
                nc.scalar.copy(out=out[:], in_=words)
            else:
                nc.scalar.copy(out=out[:, 0], in_=words[:, 0])
                nc.vector.tensor_copy(out=out[:, 1], in_=words[:, 1])
            x_sorted[(m, a)] = out

        def turn_x(j):
            bank = t_bank()
            count = len(banks_in[j])
            for c, (m, a, k) in enumerate(banks_in[j]):
                words = x_raw[m][a][:].bitcast(F32)
                for u in range(2):
                    src = x_sorted[(m, a)][:, u, k, :] if (m, a) in x_sorted else words[:, 256 * k + u:256 * (k + 1):2]
                    nc.tensor.transpose(bank[:, (2 * c + u) * P:(2 * c + u + 1) * P], src, ident[:])
            grouped = work.tile([P, count * K_PASS], BF16, name="x_grouped", align_bytes=64)
            interleave(grouped[:], bank[:, 0:count * 2 * P], count)
            state[("xg", j)] = grouped

        def quantize_x(j):
            nc.vector.quantize_mx(out=x_codes[j][:].bitcast(FP8X4), scales=x_scales[j][:], in_=state[("xg", j)][:])

        def passes(u, a, acc, n0, width):
            g, m = unit(u)
            s0 = (g - TIERS[tier_of[g]][0]) * N_GROUP + n0
            for k in range(PASSES):
                j, c = place[(m, a, k)]
                nc.tensor.matmul_mx(
                    out=acc,
                    lhsT=x_codes[j][:, c * P:(c + 1) * P].bitcast(FP8X4),
                    lhsT_scale=x_scales[j][:, c * P:(c + 1) * P],
                    rhs=w_words[a][g][:, k, 2 * n0:2 * (n0 + width)].bitcast(FP4X4),
                    rhs_scale=w_scales[a][tier_of[g]][:, k, s0:s0 + width],
                    start=(k == 0),
                    stop=(k == PASSES - 1),
                )

        def product(u, a):
            acc = psum.tile([P, N_GROUP], F32, name="acc", tag="acc%d_%d" % (a, u % 2))
            passes(u, a, acc[:], 0, N_GROUP)
            state[("acc", a, u)] = acc

        def group_cols(u):
            g = unit(u)[0]
            return slice(g * N_GROUP, (g + 1) * N_GROUP)

        def add_bias(u):
            mu = work.tile([P, N_GROUP], F32, name="mu")
            nc.vector.tensor_tensor(out=mu[:], in0=state[("acc", 0, u)][:], in1=vec_rows[0][:, group_cols(u)], op=ALU.add)
            state[("mu", u)] = mu

        def square(u):
            mu2 = work.tile([P, N_GROUP], F32, name="mu2")
            nc.scalar.activation(out=mu2[:], in_=state[("mu", u)][:], func=ACT.Square)
            state[("mu2", u)] = mu2

        def add_var(u):
            second = work.tile([P, N_GROUP], F32, name="second")
            nc.vector.tensor_tensor(out=second[:], in0=state[("acc", 1, u)][:], in1=state[("mu2", u)][:], op=ALU.add)
            state[("second", u)] = second

        def ratio(u):
            g, m = unit(u)
            engine = nc.gpsimd if u in POOL_UNITS else nc.vector
            engine.tensor_tensor(out=y[u][:], in0=state[("second", u)][:], in1=vec_rows[1][:, group_cols(u)], op=ALU.mult)
            state["stores"].append((out_0[m * P:(m + 1) * P, group_cols(u)], y[u][:]))

        def round_y(u):
            y16 = work.tile([P, N_GROUP], BF16, name="y16", bufs=6)
            nc.scalar.copy(
                out=y16[:].rearrange("p (u q e) -> p u q e", u=2, e=2),
                in_=y[u][:].rearrange("p (q u e) -> p u q e", u=2, e=2),
            )
            state[("y16", u)] = y16

        def by_word_parity(ap):
            return ap.rearrange("p (q u e) -> p u q e", u=2, e=2)

        def finish_last(u):
            g, m = unit(u)
            second = work.tile([P, 2, P, 2], F32, name="second")
            y16 = work.tile([P, N_GROUP], BF16, name="y16", bufs=6)
            inv = vec_rows[1][:, group_cols(u)]
            for h in range(2):
                nc.vector.tensor_tensor(
                    out=second[:, h], in0=by_word_parity(state[("acc", 1, u)][:])[:, h],
                    in1=by_word_parity(state[("mu2", u)][:])[:, h], op=ALU.add,
                )
            for h in range(2):
                nc.vector.tensor_tensor(
                    out=y16[:].rearrange("p (u q e) -> p u q e", u=2, e=2)[:, h],
                    in0=second[:, h], in1=by_word_parity(inv)[:, h], op=ALU.mult,
                )
            state[("second", u)] = second
            state[("y16", u)] = y16

        def ratio_last(u):
            g, m = unit(u)
            nc.vector.tensor_tensor(
                out=y[u][:].rearrange("p (q u e) -> p q u e", u=2, e=2),
                in0=state[("second", u)][:].rearrange("p u q e -> p q u e"),
                in1=vec_rows[1][:, group_cols(u)].rearrange("p (q u e) -> p q u e", u=2, e=2),
                op=ALU.mult,
            )
            state["stores"].append((out_0[m * P:(m + 1) * P, group_cols(u)], y[u][:]))

        def turn_y(u0, count):
            bank = t_bank()
            for c in range(count):
                words = state[("y16", u0 + c)][:].bitcast(F32)
                for u in range(2):
                    src = words[:, u * P:(u + 1) * P]
                    nc.tensor.transpose(bank[:, (2 * c + u) * P:(2 * c + u + 1) * P], src, ident[:])
            grouped = work.tile([P, count * N_GROUP], BF16, name="y_grouped", align_bytes=64)
            interleave(grouped[:], bank[:, 0:count * 2 * P], count)
            state[("yg", u0)] = grouped

        def quantize_y(u0, count):
            g, m = unit(u0)
            cols = slice(m * P, (m + count) * P)
            nc.vector.quantize_mx(out=y_codes[:, g, cols].bitcast(FP8X4), scales=y_scales[m // 2][:, g, (m % 2) * P:(m % 2 + count) * P], in_=state[("yg", u0)][:])
            state["stores"].append((codes_out[g, :, cols], y_codes[:, g, cols].bitcast(I32)))

        def store_scales(pair, engines):
            words = slice(pair * 2 * P // 4, (pair + 1) * 2 * P // 4)
            for q in range(4):
                engines[q % len(engines)].dma_start(
                    out=scales_out[:, 4 * q:4 * q + 4, words].rearrange("g r w -> r g w"),
                    in_=y_scales[pair][32 * q:32 * q + 4, :, :].bitcast(I32),
                )

        def flush():
            for dst, src in state["stores"]:
                nc.sync.dma_start(out=dst, in_=src)
            state["stores"].clear()

        state["stores"] = []

        make_identity(nc, ident[:])
        for first in range(len(TIERS)):
            for a in range(2):
                nc.vector.memset(w_scales[a][first][:].rearrange("p k n -> p (k n)").bitcast(I32), 0)
        nc.scalar.activation(out=warm[:, 0:1], in_=ident[:, 0:1], func=ACT.Square)
        for a in range(2):
            nc.sync.dma_start(out=vec_cols[a][:], in_=vec_hbm[a].rearrange("(p c) -> p c", p=P))
        load_x(0, 0, 0, SPLIT)
        if SPLIT < PASSES:
            load_x(0, 0, SPLIT, PASSES)
        load_x(1, 0)
        load_w(0, 0)
        load_x(0, 1)
        load_x(1, 1)
        load_w(1, 0)
        load_w(0, 1)
        load_w(1, 1)
        load_x(2, 0)
        load_x(3, 0)
        load_w(0, 2)
        load_w(1, 2)
        load_x(2, 1)
        load_x(3, 1)
        load_w(0, 3)
        load_w(1, 3)
        for a in range(2):
            load_x(4, a)
            load_x(5, a)

        def turn_and_quantize(js):
            for j in js:
                turn_x(j)
                quantize_x(j)

        def head_sort(m, a):
            if (m, a) in SORT_HEAD:
                sort_words(m, a, "vv")

        def spread_both(a, halves):
            for half in halves:
                if a == 0:
                    bank = psum.tile([P, N_GROUP], F32, name="vec_bank", tag="acc1_%d" % half)
                else:
                    bank = t_bank()
                spread(a, half, bank)
                spread_out(a, half)

        spread_both(0, (0,))
        head_sort(0, 0)
        head_sort(1, 0)
        turn_and_quantize((0,))
        if HEAD == 1:
            spread_both(0, (1,))
        turn_and_quantize((1,))
        head_sort(0, 1)
        turn_and_quantize((2,))
        if HEAD == 2:
            spread_both(0, (1,))
        product(0, 0)
        head_sort(1, 1)
        if HEAD:
            add_bias(0)
        turn_and_quantize((3, 4))
        if HEAD:
            square(0)
            spread_both(1, (0,))
        else:
            spread_both(0, (1,))
        product(1, 0)
        if HEAD:
            add_bias(1)
        turn_and_quantize((5,))
        if HEAD:
            square(1)
        else:
            spread_both(1, (0,))
            add_bias(0)
            square(0)
            add_bias(1)
            square(1)
        spread_both(1, (1,))

        turned = 6
        banks = []
        for s in range(STEPS):
            u = 2 * s
            last = s == STEPS - 1
            if s > 0:
                round_y(u - 2)
                if u - 1 not in POOL_UNITS:
                    round_y(u - 1)
                product(u, 0)
                add_bias(u)
                square(u)
                if u - 1 in POOL_UNITS:
                    round_y(u - 1)
                for j in banks[:QPOS]:
                    quantize_x(j)
                product(u + 1, 0)
                add_bias(u + 1)
                square(u + 1)
                for j in banks[QPOS:]:
                    quantize_x(j)
            if s >= 2:
                quantize_y(u - 4, 2)
            product(u, 1)
            add_var(u)
            if last:
                ratio(u)
                product(u + 1, 1)
                if TAIL == 0:
                    turn_y(u - 2, 2)
                    round_y(u)
                else:
                    round_y(u)
                    turn_y(u - 2, 2)
                finish_last(u + 1)
                turn_y(u, 1)
                turn_y(u + 1, 1)
                quantize_y(u - 2, 2)
                ratio_last(u + 1)
                quantize_y(u, 1)
                quantize_y(u + 1, 1)
                flush()
                store_scales(2, (nc.scalar, nc.sync))
            else:
                if u in POOL_UNITS:
                    ratio(u)
                product(u + 1, 1)
                add_var(u + 1)
                if u not in POOL_UNITS:
                    ratio(u)
                ratio(u + 1)
                banks = list(range(turned, turned + IN_RUNS.get(s + 1, 0)))
                turned = turned + len(banks)
                for j in banks:
                    turn_x(j)
                if s >= 1:
                    turn_y(u - 2, 2)
                flush()
                if s in (GROUPS + 1, 2 * GROUPS + 1):
                    store_scales(s // GROUPS - 1, (nc.sync,))
